import numpy as np
import ml_dtypes


def mxq(x, axis, fmt="e4m3"):
    dtype, down = {"e4m3": (ml_dtypes.float8_e4m3fn, 7), "e5m2": (ml_dtypes.float8_e5m2, 14)}[fmt]
    v = np.moveaxis(np.asarray(x, np.float32).astype(ml_dtypes.bfloat16).astype(np.float64), axis, -1)
    blocks = v.reshape(v.shape[:-1] + (-1, 32))
    amax = np.abs(blocks).max(-1, keepdims=True)
    byte = np.maximum(np.where(amax > 0, np.frexp(amax)[1] - 1 + 127, 0) - down, 1)
    scale = np.exp2(byte - 127.0)
    codes = (blocks / scale).astype(np.float32).astype(dtype).astype(np.float64)
    return np.moveaxis((codes * scale).reshape(v.shape), -1, axis)


WIDE = False


def mx_kscale(k, group=512):
    if not WIDE:
        return np.ones(k)
    levels = np.array([10, -10, 5, -5, 0])
    if group != 512:
        return np.exp2(np.random.permutation(np.resize(levels, k // group))).repeat(group)
    if k % 512:
        return np.exp2(np.random.permutation(np.resize(levels, k // 32))).repeat(32)
    a = np.empty((k // 512, 16))
    for p in range(k // 512):
        a[p, :8] = np.random.permutation(np.resize(levels, 8))
        for g in range(8):
            far = levels[np.abs(levels - a[p, g]) >= 10]
            a[p, g + 8] = far[np.random.randint(len(far))]
    return np.exp2(a.ravel()).repeat(32)


def f64(x):
    return np.asarray(x).astype(np.float64)


E2M1 = np.array([0.0, 0.5, 1.0, 1.5, 2.0, 3.0, 4.0, 6.0, -0.0, -0.5, -1.0, -1.5, -2.0, -3.0, -4.0, -6.0])


def pack_group(w):
    k, n = w.shape
    w = f64(np.asarray(w, np.float32).astype(ml_dtypes.bfloat16)).reshape(k // 32, 32, n)
    amax = np.abs(w).max(1)
    mant, ex = np.frexp(amax / 6.0)
    byte = np.clip(np.where(amax > 0, np.where(mant > 0.5, ex, ex - 1) + 127, 1), 1, 254)
    scaled = (w * np.exp2(127.0 - byte)[:, None, :]).reshape(k, n).astype(np.float32)
    c = np.ascontiguousarray(scaled.reshape(k // 4, 4, n).transpose(0, 2, 1)).astype(ml_dtypes.float4_e2m1fn).view(np.uint8) & 0xF
    return np.ascontiguousarray((c[..., 0::2] | (c[..., 1::2] << 4)).reshape(k // 4, 2 * n)), byte.astype(np.uint8)


def unpack_group(words, scales):
    p, n = words.shape[0], scales.shape[1]
    words = np.ascontiguousarray(words).reshape(p, n, 2)
    nib = np.empty((p, n, 4), np.uint8)
    nib[..., 0::2] = words & 0xF
    nib[..., 1::2] = words >> 4
    return E2M1[nib].transpose(0, 2, 1).reshape(4 * p, n) * np.repeat(np.exp2(scales.astype(np.float64) - 127.0), 32, axis=0)


def softplus(v):
    return np.log(1.0 + np.exp(v))


def sigmoid(v):
    return 1.0 / (1.0 + np.exp(-v))


G, D, M, O, N = 2, 256, 256, 256, 512


def setup_inputs():
    n = np.random.standard_normal
    s_d = mx_kscale(D, 0)
    s_o = mx_kscale(O, 0)
    w1_ = [pack_group(w) for w in n((G, D, M)) / np.sqrt(D) / s_d[:, None]]
    w2_ = [pack_group(w) for w in n((G, D, M)) / np.sqrt(D) / s_d[:, None]]
    wo_ = [pack_group(w) for w in n((G, O, M)) / np.sqrt(O) / s_o[:, None]]
    return {
        "x": (n((G, D, N)) * s_d[:, None]).astype(np.float32),
        "w1_words": np.stack([w[0] for w in w1_]),
        "w1_scales": np.stack([w[1] for w in w1_]),
        "w2_words": np.stack([w[0] for w in w2_]),
        "w2_scales": np.stack([w[1] for w in w2_]),
        "hp1": (np.random.uniform(0.3, 1.0, (G, M, 1))).astype(np.float32),
        "wo_words": np.stack([w[0] for w in wo_]),
        "wo_scales": np.stack([w[1] for w in wo_]),
        "dy": (n((G, O, N)) * s_o[:, None]).astype(np.float32),
        "old": (0.3 * n((G, M, N))).astype(np.float32),
    }


def reference(x, w1_words, w1_scales, w2_words, w2_scales, hp1, wo_words, wo_scales, dy, old):
    w1 = np.stack([unpack_group(w1_words[g], w1_scales[g]) for g in range(G)])
    xq = mxq(f64(x), 1, "e4m3")
    z1 = w1.transpose(0, 2, 1) @ xq
    w2 = np.stack([unpack_group(w2_words[g], w2_scales[g]) for g in range(G)])
    z2 = w2.transpose(0, 2, 1) @ xq
    q1 = np.square(softplus(z1))
    wo = np.stack([unpack_group(wo_words[g], wo_scales[g]) for g in range(G)])
    dyq = mxq(f64(dy), 1, "e4m3")
    c0 = wo.transpose(0, 2, 1) @ dyq
    dq1 = c0 * 2.0 / (q1 + softplus(z2) + f64(hp1)) - c0 * 2.0 * q1 / np.square(q1 + softplus(z2) + f64(hp1))
    dz1 = dq1 * softplus(z1) * 2.0 * sigmoid(z1)
    y = dz1 + f64(old)
    return y

@@ -1,0 +1,197 @@
+from contextlib import ExitStack
+
+import concourse.mybir as mybir
+
+G, D, M, N = 2, 256, 256, 512
+FLOPS = 3 * 2 * G * D * M * N
+
+F32 = mybir.dt.float32
+BF16 = mybir.dt.bfloat16
+I32 = mybir.dt.int32
+U32 = mybir.dt.uint32
+U8 = mybir.dt.uint8
+FP8X4 = mybir.dt.float8_e4m3fn_x4
+FP4X4 = mybir.dt.float4_e2m1fn_x4
+ACT = mybir.ActivationFunctionType
+ALU = mybir.AluOpType
+
+P = 128
+PACK = 4
+ROWS = D // PACK
+HALVES = M // P
+TILES = [(g, t) for t in range(HALVES) for g in range(G)]
+LN_FLOOR = 2.0 ** -50
+X_SPLIT = 336
+
+
+def tile_rows_bhill_kernel(tc, x, w1_words, w1_scales, w2_words, w2_scales, hp1, wo_words, wo_scales, dy, old, out):
+    nc = tc.nc
+    with ExitStack() as ctx:
+        sb = ctx.enter_context(tc.tile_pool(name="sb", bufs=1))
+        ps = ctx.enter_context(tc.psum_pool(name="ps", bufs=1))
+        ctx.enter_context(tc.manual_schedule())
+
+        def per_tile(name):
+            return [sb.tile([P, N], F32, name=f"{name}{i}") for i in range(len(TILES))]
+
+        w_scales = sb.tile([P, 3, M], U8, name="w_scales", align_bytes=64)
+        w_words = [sb.tile([P, 2 * M], U8, name=f"w_words{w}", align_bytes=64) for w in range(3)]
+        raw = [sb.tile([P, PACK, N], F32, name=f"raw{a}") for a in range(2)]
+        packed = [sb.tile([P, N, PACK], BF16, name=f"packed{a}", align_bytes=64) for a in range(2)]
+        codes = [sb.tile([P, N], U32, name=f"codes{a}", align_bytes=64) for a in range(2)]
+        scales = [sb.tile([P, N], U8, name=f"scales{a}", align_bytes=64) for a in range(2)]
+        half_point = sb.tile([P, G * HALVES, 8], F32, name="half_point")
+        old_sb = sb.tile([P, G * HALVES, N], F32, name="old_sb")
+        warm = sb.tile([P, 2], F32, name="warm")
+        bank1 = [ps.tile([P, N], F32, name=f"bank1_{i}") for i in range(len(TILES))]
+        bank2 = [ps.tile([P, N], F32, name=f"bank2_{i}") for i in range(len(TILES))]
+        t1, t2, l1, l2, n1, n2, q, den, lden, inv2, a, prod, b, dz, res = [
+            per_tile(s)
+            for s in ("t1", "t2", "l1", "l2", "n1", "n2", "q", "den", "lden", "inv2", "a", "prod", "b", "dz", "res")
+        ]
+
+        def load_weight(w, words, scale_bytes):
+            nc.sync.dma_start(out=w_words[w][:].bitcast(I32), in_=words.rearrange("g p b -> (g p) b").bitcast(I32))
+            rows = scale_bytes.rearrange("g t m -> (g t) m").bitcast(I32)
+            for quad in range(4):
+                nc.sync.dma_start(
+                    out=w_scales[32 * quad : 32 * quad + 4, w, :].bitcast(I32), in_=rows[4 * quad : 4 * quad + 4, :]
+                )
+
+        def load_act(k, src):
+            nc.sync.dma_start(out=raw[k][:], in_=src.rearrange("g (p j) n -> (g p) j n", j=PACK))
+
+        def interleave_views(k, c0, c1):
+            dst = packed[k][:, c0:c1, :].rearrange("p (c i) j -> p c j i", i=4)
+            src = raw[k][:, :, c0:c1].rearrange("p j (c i) -> p c j i", i=4)
+            return dst, src
+
+        def quantize(k):
+            nc.vector.quantize_mx(
+                out=codes[k][:].bitcast(FP8X4), scales=scales[k][:], in_=packed[k][:].rearrange("p n j -> p (n j)")
+            )
+
+        def product(bank, i, w, k):
+            g, t = TILES[i]
+            rows = slice(ROWS * g, ROWS * (g + 1))
+            nc.tensor.matmul_mx(
+                out=bank[:],
+                lhsT=w_words[w][rows, 2 * P * t : 2 * P * (t + 1)].bitcast(FP4X4),
+                lhsT_scale=w_scales[rows, w, P * t : P * (t + 1)],
+                rhs=codes[k][rows, :].bitcast(FP8X4),
+                rhs_scale=scales[k][rows, :],
+                start=True,
+                stop=True,
+            )
+
+        def h(i):
+            g, t = TILES[i]
+            return half_point[:, HALVES * g + t, 0:1]
+
+        def stt(dst, in0, scalar, in1, op0, op1):
+            nc.vector.scalar_tensor_tensor(out=dst[:], in0=in0[:], scalar=scalar, in1=in1[:], op0=op0, op1=op1)
+
+        nc.vector.memset(w_scales[:].rearrange("p w m -> p (w m)").bitcast(I32), 0)
+        nc.vector.memset(warm[:, 0:1], 0.0)
+        nc.scalar.activation(out=warm[:, 1:2], in_=warm[:, 0:1], func=ACT.Sigmoid)
+
+        load_act(0, x)
+        load_weight(0, w1_words, w1_scales)
+        load_weight(1, w2_words, w2_scales)
+        load_act(1, dy)
+        load_weight(2, wo_words, wo_scales)
+        with nc.allow_non_contiguous_dma(reason="one half point a partition"):
+            nc.sync.dma_start(out=half_point[:, :, 0:1], in_=hp1.rearrange("g (t p) o -> p (g t) o", p=P))
+        nc.sync.dma_start(out=old_sb[:], in_=old.rearrange("g (t p) n -> p (g t) n", p=P))
+
+        dst, src = interleave_views(0, 0, X_SPLIT)
+        nc.vector.tensor_copy(out=dst, in_=src)
+        dst, src = interleave_views(0, X_SPLIT, N)
+        nc.scalar.copy(out=dst, in_=src)
+        quantize(0)
+        tiles = range(len(TILES))
+        late_first = [2, 3, 0, 1]
+        for i in late_first:
+            product(bank1[i], i, 0, 0)
+            nc.scalar.activation(out=t1[i][:], in_=bank1[i][:], func=ACT.Sigmoid, scale=-1.0)
+        for i in late_first:
+            product(bank2[i], i, 1, 0)
+            nc.scalar.activation(out=t2[i][:], in_=bank2[i][:], func=ACT.Sigmoid, scale=-1.0)
+
+        dst, src = interleave_views(1, 0, N)
+        nc.vector.tensor_copy(out=dst, in_=src)
+        quantize(1)
+        c0_bank = {2: bank1[2], 3: bank1[3], 0: bank2[2], 1: bank2[3]}
+        for i in late_first:
+            product(c0_bank[i], i, 2, 1)
+            stt(a[i], t1[i], 1.0, c0_bank[i], ALU.subtract, ALU.mult)
+        for i in (2, 3):
+            product(bank1[i], i, 0, 0)
+            product(bank2[i], i, 1, 0)
+
+        def s_l1(i):
+            nc.scalar.activation(out=l1[i][:], in_=t1[i][:], func=ACT.Ln, bias=LN_FLOOR)
+
+        def s_l2(i):
+            nc.scalar.activation(out=l2[i][:], in_=t2[i][:], func=ACT.Ln, bias=LN_FLOOR)
+
+        def s_q(i):
+            nc.scalar.activation(out=q[i][:], in_=n1[i][:], func=ACT.Square)
+
+        def s_lden(i):
+            nc.scalar.activation(out=lden[i][:], in_=den[i][:], func=ACT.Ln)
+
+        def s_inv2(i):
+            nc.scalar.activation(out=inv2[i][:], in_=lden[i][:], func=ACT.Exp, scale=-2.0)
+
+        def v_n1(i):
+            stt(n1[i], bank1[i], -1.0, l1[i], ALU.mult, ALU.min)
+
+        def v_n2(i):
+            stt(n2[i], bank2[i], -1.0, l2[i], ALU.mult, ALU.min)
+
+        def v_den(i):
+            stt(den[i], q[i], h(i), n2[i], ALU.add, ALU.subtract)
+
+        def v_prod(i):
+            stt(prod[i], n2[i], h(i), n1[i], ALU.subtract, ALU.mult)
+
+        def v_b(i):
+            stt(b[i], a[i], -4.0, prod[i], ALU.mult, ALU.mult)
+
+        def v_dz(i):
+            nc.vector.tensor_tensor(out=dz[i][:], in0=b[i][:], in1=inv2[i][:], op=ALU.mult)
+
+        def v_res(i, c0, c1):
+            g, t = TILES[i]
+            nc.vector.tensor_tensor(
+                out=res[i][:, c0:c1], in0=dz[i][:, c0:c1], in1=old_sb[:, HALVES * g + t, c0:c1], op=ALU.add
+            )
+            nc.sync.dma_start(out=out[g, P * t : P * (t + 1), c0:c1], in_=res[i][:, c0:c1])
+
+        count = len(TILES)
+        for step in range(count + 2):
+            if step < count:
+                s_l1(step)
+                s_l2(step)
+                v_n1(step)
+                v_n2(step)
+            if 1 <= step <= count:
+                s_q(step - 1)
+                v_den(step - 1)
+            if step >= 2:
+                s_lden(step - 2)
+            if 1 <= step <= 2:
+                v_prod(step - 1)
+        v_prod(2)
+        v_prod(3)
+        for i in tiles:
+            v_b(i)
+        for i in tiles:
+            s_inv2(i)
+        for step in range(count):
+            v_dz(step)
+            if step >= 1:
+                v_res(step - 1, 0, N)
+        v_res(count - 1, 0, N // 2)
+        v_res(count - 1, N // 2, N)

@@ -32,7 +32,7 @@ def tile_rows_bhill_kernel(tc, x, w1_words, w1_scales, w2_words, w2_scales, hp1,
         ctx.enter_context(tc.manual_schedule())
 
         def per_tile(name):
-            return [sb.tile([P, N], F32, name=f"{name}{i}") for i in range(len(TILES))]
+            return sb.tile([P, len(TILES) * N], F32, name=name)
 
         w_scales = sb.tile([P, 3, M], U8, name="w_scales", align_bytes=64)
         w_words = [sb.tile([P, 2 * M], U8, name=f"w_words{w}", align_bytes=64) for w in range(3)]
@@ -41,7 +41,7 @@ def tile_rows_bhill_kernel(tc, x, w1_words, w1_scales, w2_words, w2_scales, hp1,
         codes = [sb.tile([P, N], U32, name=f"codes{a}", align_bytes=64) for a in range(2)]
         scales = [sb.tile([P, N], U8, name=f"scales{a}", align_bytes=64) for a in range(2)]
         half_point = sb.tile([P, G * HALVES, 8], F32, name="half_point")
-        old_sb = sb.tile([P, G * HALVES, N], F32, name="old_sb")
+        old_sb = sb.tile([P, HALVES, G, N], F32, name="old_sb")
         warm = sb.tile([P, 2], F32, name="warm")
         bank1 = [ps.tile([P, N], F32, name=f"bank1_{i}") for i in range(len(TILES))]
         bank2 = [ps.tile([P, N], F32, name=f"bank2_{i}") for i in range(len(TILES))]
@@ -50,8 +50,10 @@ def tile_rows_bhill_kernel(tc, x, w1_words, w1_scales, w2_words, w2_scales, hp1,
             for s in ("t1", "t2", "l1", "l2", "n1", "n2", "q", "den", "lden", "inv2", "a", "prod", "b", "dz", "res")
         ]
 
-        def load_weight(w, words, scale_bytes):
+        def load_words(w, words):
             nc.sync.dma_start(out=w_words[w][:].bitcast(I32), in_=words.rearrange("g p b -> (g p) b").bitcast(I32))
+
+        def load_scales(w, scale_bytes):
             rows = scale_bytes.rearrange("g t m -> (g t) m").bitcast(I32)
             for quad in range(4):
                 nc.sync.dma_start(
@@ -88,21 +90,28 @@ def tile_rows_bhill_kernel(tc, x, w1_words, w1_scales, w2_words, w2_scales, hp1,
             g, t = TILES[i]
             return half_point[:, HALVES * g + t, 0:1]
 
+        def cols(i, c0=0, c1=N):
+            return slice(i * N + c0, i * N + c1)
+
         def stt(dst, in0, scalar, in1, op0, op1):
-            nc.vector.scalar_tensor_tensor(out=dst[:], in0=in0[:], scalar=scalar, in1=in1[:], op0=op0, op1=op1)
+            nc.vector.scalar_tensor_tensor(out=dst, in0=in0, scalar=scalar, in1=in1, op0=op0, op1=op1)
 
         nc.vector.memset(w_scales[:].rearrange("p w m -> p (w m)").bitcast(I32), 0)
         nc.vector.memset(warm[:, 0:1], 0.0)
         nc.scalar.activation(out=warm[:, 1:2], in_=warm[:, 0:1], func=ACT.Sigmoid)
 
         load_act(0, x)
-        load_weight(0, w1_words, w1_scales)
-        load_weight(1, w2_words, w2_scales)
+        load_words(0, w1_words)
+        load_scales(0, w1_scales)
+        load_words(1, w2_words)
         load_act(1, dy)
-        load_weight(2, wo_words, wo_scales)
+        load_scales(1, w2_scales)
+        load_words(2, wo_words)
+        load_scales(2, wo_scales)
         with nc.allow_non_contiguous_dma(reason="one half point a partition"):
             nc.sync.dma_start(out=half_point[:, :, 0:1], in_=hp1.rearrange("g (t p) o -> p (g t) o", p=P))
-        nc.sync.dma_start(out=old_sb[:], in_=old.rearrange("g (t p) n -> p (g t) n", p=P))
+        for t in range(HALVES):
+            nc.sync.dma_start(out=old_sb[:, t], in_=old[:, P * t : P * (t + 1), :].rearrange("g p n -> p g n"))
 
         dst, src = interleave_views(0, 0, X_SPLIT)
         nc.vector.tensor_copy(out=dst, in_=src)
@@ -113,10 +122,10 @@ def tile_rows_bhill_kernel(tc, x, w1_words, w1_scales, w2_words, w2_scales, hp1,
         late_first = [2, 3, 0, 1]
         for i in late_first:
             product(bank1[i], i, 0, 0)
-            nc.scalar.activation(out=t1[i][:], in_=bank1[i][:], func=ACT.Sigmoid, scale=-1.0)
+            nc.scalar.activation(out=t1[:, cols(i)], in_=bank1[i][:], func=ACT.Sigmoid, scale=-1.0)
         for i in late_first:
             product(bank2[i], i, 1, 0)
-            nc.scalar.activation(out=t2[i][:], in_=bank2[i][:], func=ACT.Sigmoid, scale=-1.0)
+            nc.scalar.activation(out=t2[:, cols(i)], in_=bank2[i][:], func=ACT.Sigmoid, scale=-1.0)
 
         dst, src = interleave_views(1, 0, N)
         nc.vector.tensor_copy(out=dst, in_=src)
@@ -124,74 +133,61 @@ def tile_rows_bhill_kernel(tc, x, w1_words, w1_scales, w2_words, w2_scales, hp1,
         c0_bank = {2: bank1[2], 3: bank1[3], 0: bank2[2], 1: bank2[3]}
         for i in late_first:
             product(c0_bank[i], i, 2, 1)
-            stt(a[i], t1[i], 1.0, c0_bank[i], ALU.subtract, ALU.mult)
+            stt(a[:, cols(i)], t1[:, cols(i)], 1.0, c0_bank[i][:], ALU.subtract, ALU.mult)
         for i in (2, 3):
             product(bank1[i], i, 0, 0)
             product(bank2[i], i, 1, 0)
 
-        def s_l1(i):
-            nc.scalar.activation(out=l1[i][:], in_=t1[i][:], func=ACT.Ln, bias=LN_FLOOR)
+        old_flat = old_sb[:].rearrange("p t g n -> p (t g n)")
 
-        def s_l2(i):
-            nc.scalar.activation(out=l2[i][:], in_=t2[i][:], func=ACT.Ln, bias=LN_FLOOR)
+        def s_ln(dst, src, where, bias):
+            nc.scalar.activation(out=dst[:, where], in_=src[:, where], func=ACT.Ln, bias=bias)
 
-        def s_q(i):
-            nc.scalar.activation(out=q[i][:], in_=n1[i][:], func=ACT.Square)
-
-        def s_lden(i):
-            nc.scalar.activation(out=lden[i][:], in_=den[i][:], func=ACT.Ln)
-
-        def s_inv2(i):
-            nc.scalar.activation(out=inv2[i][:], in_=lden[i][:], func=ACT.Exp, scale=-2.0)
-
-        def v_n1(i):
-            stt(n1[i], bank1[i], -1.0, l1[i], ALU.mult, ALU.min)
-
-        def v_n2(i):
-            stt(n2[i], bank2[i], -1.0, l2[i], ALU.mult, ALU.min)
-
-        def v_den(i):
-            stt(den[i], q[i], h(i), n2[i], ALU.add, ALU.subtract)
+        def v_min(dst, bank, src, i, c0=0, c1=N):
+            stt(dst[:, cols(i, c0, c1)], bank[i][:, c0:c1], -1.0, src[:, cols(i, c0, c1)], ALU.mult, ALU.min)
 
         def v_prod(i):
-            stt(prod[i], n2[i], h(i), n1[i], ALU.subtract, ALU.mult)
+            stt(prod[:, cols(i)], n2[:, cols(i)], h(i), n1[:, cols(i)], ALU.subtract, ALU.mult)
 
-        def v_b(i):
-            stt(b[i], a[i], -4.0, prod[i], ALU.mult, ALU.mult)
+        def s_inv2(where):
+            nc.scalar.activation(out=inv2[:, where], in_=lden[:, where], func=ACT.Exp, scale=-2.0)
 
-        def v_dz(i):
-            nc.vector.tensor_tensor(out=dz[i][:], in0=b[i][:], in1=inv2[i][:], op=ALU.mult)
+        def v_dz(where):
+            nc.vector.tensor_tensor(out=dz[:, where], in0=b[:, where], in1=inv2[:, where], op=ALU.mult)
 
-        def v_res(i, c0, c1):
+        def v_res(i, c0=0, c1=N):
             g, t = TILES[i]
-            nc.vector.tensor_tensor(
-                out=res[i][:, c0:c1], in0=dz[i][:, c0:c1], in1=old_sb[:, HALVES * g + t, c0:c1], op=ALU.add
-            )
-            nc.sync.dma_start(out=out[g, P * t : P * (t + 1), c0:c1], in_=res[i][:, c0:c1])
+            where = cols(i, c0, c1)
+            nc.vector.tensor_tensor(out=res[:, where], in0=dz[:, where], in1=old_flat[:, where], op=ALU.add)
+            nc.sync.dma_start(out=out[g, P * t : P * (t + 1), c0:c1], in_=res[:, where])
 
         count = len(TILES)
         for step in range(count + 2):
             if step < count:
-                s_l1(step)
-                s_l2(step)
-                v_n1(step)
-                v_n2(step)
+                pieces = [(0, N // 2), (N // 2, N)] if step == 0 else [(0, N)]
+                for c0, c1 in pieces:
+                    s_ln(l1, t1, cols(step, c0, c1), LN_FLOOR)
+                    v_min(n1, bank1, l1, step, c0, c1)
+                s_ln(l2, t2, cols(step), LN_FLOOR)
+                v_min(n2, bank2, l2, step)
             if 1 <= step <= count:
-                s_q(step - 1)
-                v_den(step - 1)
+                i = step - 1
+                nc.scalar.activation(out=q[:, cols(i)], in_=n1[:, cols(i)], func=ACT.Square)
+                stt(den[:, cols(i)], q[:, cols(i)], h(i), n2[:, cols(i)], ALU.add, ALU.subtract)
             if step >= 2:
-                s_lden(step - 2)
+                s_ln(lden, den, cols(step - 2), 0.0)
             if 1 <= step <= 2:
                 v_prod(step - 1)
         v_prod(2)
         v_prod(3)
+        for pair in range(2):
+            where = slice(2 * pair * N, 2 * (pair + 1) * N)
+            stt(b[:, where], a[:, where], -4.0, prod[:, where], ALU.mult, ALU.mult)
         for i in tiles:
-            v_b(i)
-        for i in tiles:
-            s_inv2(i)
+            s_inv2(cols(i))
         for step in range(count):
-            v_dz(step)
+            v_dz(cols(step))
             if step >= 1:
-                v_res(step - 1, 0, N)
+                v_res(step - 1)
         v_res(count - 1, 0, N // 2)
         v_res(count - 1, N // 2, N)

@@ -22,6 +22,7 @@ HALVES = M // P
 TILES = [(g, t) for t in range(HALVES) for g in range(G)]
 LN_FLOOR = 2.0 ** -50
 X_SPLIT = 336
+POOL_COLS = 768
 
 
 def tile_rows_bhill_kernel(tc, x, w1_words, w1_scales, w2_words, w2_scales, hp1, wo_words, wo_scales, dy, old, out):
@@ -136,6 +137,7 @@ def tile_rows_bhill_kernel(tc, x, w1_words, w1_scales, w2_words, w2_scales, hp1,
             stt(a[:, cols(i)], t1[:, cols(i)], 1.0, c0_bank[i][:], ALU.subtract, ALU.mult)
         for i in (2, 3):
             product(bank1[i], i, 0, 0)
+        for i in (2, 3):
             product(bank2[i], i, 1, 0)
 
         old_flat = old_sb[:].rearrange("p t g n -> p (t g n)")
@@ -146,14 +148,14 @@ def tile_rows_bhill_kernel(tc, x, w1_words, w1_scales, w2_words, w2_scales, hp1,
         def v_min(dst, bank, src, i, c0=0, c1=N):
             stt(dst[:, cols(i, c0, c1)], bank[i][:, c0:c1], -1.0, src[:, cols(i, c0, c1)], ALU.mult, ALU.min)
 
-        def v_prod(i):
-            stt(prod[:, cols(i)], n2[:, cols(i)], h(i), n1[:, cols(i)], ALU.subtract, ALU.mult)
+        def mul(engine, dst, in0, in1, where):
+            engine.tensor_tensor(out=dst[:, where], in0=in0[:, where], in1=in1[:, where], op=ALU.mult)
 
         def s_inv2(where):
             nc.scalar.activation(out=inv2[:, where], in_=lden[:, where], func=ACT.Exp, scale=-2.0)
 
         def v_dz(where):
-            nc.vector.tensor_tensor(out=dz[:, where], in0=b[:, where], in1=inv2[:, where], op=ALU.mult)
+            stt(dz[:, where], b[:, where], -4.0, inv2[:, where], ALU.mult, ALU.mult)
 
         def v_res(i, c0=0, c1=N):
             g, t = TILES[i]
@@ -162,27 +164,24 @@ def tile_rows_bhill_kernel(tc, x, w1_words, w1_scales, w2_words, w2_scales, hp1,
             nc.sync.dma_start(out=out[g, P * t : P * (t + 1), c0:c1], in_=res[:, where])
 
         count = len(TILES)
-        for step in range(count + 2):
-            if step < count:
-                pieces = [(0, N // 2), (N // 2, N)] if step == 0 else [(0, N)]
-                for c0, c1 in pieces:
-                    s_ln(l1, t1, cols(step, c0, c1), LN_FLOOR)
-                    v_min(n1, bank1, l1, step, c0, c1)
-                s_ln(l2, t2, cols(step), LN_FLOOR)
-                v_min(n2, bank2, l2, step)
-            if 1 <= step <= count:
-                i = step - 1
+        for i in tiles:
+            for c0, c1 in [(0, N // 2), (N // 2, N)] if i == 0 else [(0, N)]:
+                s_ln(l1, t1, cols(i, c0, c1), LN_FLOOR)
+                v_min(n1, bank1, l1, i, c0, c1)
+        mul(nc.gpsimd, q, n1, n1, cols(0))
+        mul(nc.gpsimd, prod, a, n1, slice(0, POOL_COLS))
+        for i in tiles:
+            s_ln(l2, t2, cols(i), LN_FLOOR)
+            v_min(n2, bank2, l2, i)
+        for i in tiles:
+            if i > 0:
                 nc.scalar.activation(out=q[:, cols(i)], in_=n1[:, cols(i)], func=ACT.Square)
-                stt(den[:, cols(i)], q[:, cols(i)], h(i), n2[:, cols(i)], ALU.add, ALU.subtract)
-            if step >= 2:
-                s_ln(lden, den, cols(step - 2), 0.0)
-            if 1 <= step <= 2:
-                v_prod(step - 1)
-        v_prod(2)
-        v_prod(3)
-        for pair in range(2):
-            where = slice(2 * pair * N, 2 * (pair + 1) * N)
-            stt(b[:, where], a[:, where], -4.0, prod[:, where], ALU.mult, ALU.mult)
+            stt(den[:, cols(i)], q[:, cols(i)], h(i), n2[:, cols(i)], ALU.add, ALU.subtract)
+        for i in tiles:
+            s_ln(lden, den, cols(i), 0.0)
+        mul(nc.vector, prod, a, n1, slice(POOL_COLS, count * N))
+        for i in tiles:
+            stt(b[:, cols(i)], n2[:, cols(i)], h(i), prod[:, cols(i)], ALU.subtract, ALU.mult)
         for i in tiles:
             s_inv2(cols(i))
         for step in range(count):

@@ -20,9 +20,9 @@ PACK = 4
 ROWS = D // PACK
 HALVES = M // P
 TILES = [(g, t) for t in range(HALVES) for g in range(G)]
-LN_FLOOR = 2.0 ** -50
-X_SPLIT = 336
-POOL_COLS = 768
+CROSSOVER = 35.0
+X_SPLIT = 304
+POOL_COLS = 896
 
 
 def tile_rows_bhill_kernel(tc, x, w1_words, w1_scales, w2_words, w2_scales, hp1, wo_words, wo_scales, dy, old, out):
@@ -69,9 +69,11 @@ def tile_rows_bhill_kernel(tc, x, w1_words, w1_scales, w2_words, w2_scales, hp1,
             src = raw[k][:, :, c0:c1].rearrange("p j (c i) -> p c j i", i=4)
             return dst, src
 
-        def quantize(k):
+        def quantize(k, c0, c1):
             nc.vector.quantize_mx(
-                out=codes[k][:].bitcast(FP8X4), scales=scales[k][:], in_=packed[k][:].rearrange("p n j -> p (n j)")
+                out=codes[k][:, c0:c1].bitcast(FP8X4),
+                scales=scales[k][:, c0:c1],
+                in_=packed[k][:, c0:c1, :].rearrange("p n j -> p (n j)"),
             )
 
         def product(bank, i, w, k):
@@ -98,9 +100,10 @@ def tile_rows_bhill_kernel(tc, x, w1_words, w1_scales, w2_words, w2_scales, hp1,
             nc.vector.scalar_tensor_tensor(out=dst, in0=in0, scalar=scalar, in1=in1, op0=op0, op1=op1)
 
         nc.vector.memset(w_scales[:].rearrange("p w m -> p (w m)").bitcast(I32), 0)
-        nc.vector.memset(warm[:, 0:1], 0.0)
+        nc.vector.memset(warm[:, 0:1], -CROSSOVER)
         nc.scalar.activation(out=warm[:, 1:2], in_=warm[:, 0:1], func=ACT.Sigmoid)
 
+        floor = warm[:, 1:2]
         load_act(0, x)
         load_words(0, w1_words)
         load_scales(0, w1_scales)
@@ -114,11 +117,13 @@ def tile_rows_bhill_kernel(tc, x, w1_words, w1_scales, w2_words, w2_scales, hp1,
         for t in range(HALVES):
             nc.sync.dma_start(out=old_sb[:, t], in_=old[:, P * t : P * (t + 1), :].rearrange("g p n -> p g n"))
 
-        dst, src = interleave_views(0, 0, X_SPLIT)
-        nc.vector.tensor_copy(out=dst, in_=src)
+        for c0, c1 in ((0, N // 2), (N // 2, X_SPLIT)):
+            dst, src = interleave_views(0, c0, c1)
+            nc.vector.tensor_copy(out=dst, in_=src)
         dst, src = interleave_views(0, X_SPLIT, N)
         nc.scalar.copy(out=dst, in_=src)
-        quantize(0)
+        quantize(0, 0, N // 2)
+        quantize(0, N // 2, N)
         tiles = range(len(TILES))
         late_first = [2, 3, 0, 1]
         for i in late_first:
@@ -130,7 +135,7 @@ def tile_rows_bhill_kernel(tc, x, w1_words, w1_scales, w2_words, w2_scales, hp1,
 
         dst, src = interleave_views(1, 0, N)
         nc.vector.tensor_copy(out=dst, in_=src)
-        quantize(1)
+        quantize(1, 0, N)
         c0_bank = {2: bank1[2], 3: bank1[3], 0: bank2[2], 1: bank2[3]}
         for i in late_first:
             product(c0_bank[i], i, 2, 1)
@@ -166,12 +171,12 @@ def tile_rows_bhill_kernel(tc, x, w1_words, w1_scales, w2_words, w2_scales, hp1,
         count = len(TILES)
         for i in tiles:
             for c0, c1 in [(0, N // 2), (N // 2, N)] if i == 0 else [(0, N)]:
-                s_ln(l1, t1, cols(i, c0, c1), LN_FLOOR)
+                s_ln(l1, t1, cols(i, c0, c1), floor)
                 v_min(n1, bank1, l1, i, c0, c1)
         mul(nc.gpsimd, q, n1, n1, cols(0))
         mul(nc.gpsimd, prod, a, n1, slice(0, POOL_COLS))
         for i in tiles:
-            s_ln(l2, t2, cols(i), LN_FLOOR)
+            s_ln(l2, t2, cols(i), floor)
             v_min(n2, bank2, l2, i)
         for i in tiles:
             if i > 0:
@@ -182,11 +187,18 @@ def tile_rows_bhill_kernel(tc, x, w1_words, w1_scales, w2_words, w2_scales, hp1,
         mul(nc.vector, prod, a, n1, slice(POOL_COLS, count * N))
         for i in tiles:
             stt(b[:, cols(i)], n2[:, cols(i)], h(i), prod[:, cols(i)], ALU.subtract, ALU.mult)
+        halves = [(0, N // 2), (N // 2, N)]
+        last = count - 1
         for i in tiles:
-            s_inv2(cols(i))
-        for step in range(count):
-            v_dz(cols(step))
-            if step >= 1:
-                v_res(step - 1)
-        v_res(count - 1, 0, N // 2)
-        v_res(count - 1, N // 2, N)
+            for c0, c1 in halves if i == 0 else [(0, N)]:
+                s_inv2(cols(i, c0, c1))
+        for c0, c1 in halves:
+            v_dz(cols(0, c0, c1))
+        for i in range(1, last):
+            v_dz(cols(i))
+            v_res(i - 1)
+        v_dz(cols(last, *halves[0]))
+        v_res(last - 1)
+        v_dz(cols(last, *halves[1]))
+        for c0, c1 in halves:
+            v_res(last, c0, c1)

@@ -21,7 +21,7 @@ ROWS = D // PACK
 HALVES = M // P
 TILES = [(g, t) for t in range(HALVES) for g in range(G)]
 CROSSOVER = 35.0
-X_SPLIT = 304
+X_SPLIT = 416
 POOL_COLS = 896
 
 
@@ -37,7 +37,8 @@ def tile_rows_bhill_kernel(tc, x, w1_words, w1_scales, w2_words, w2_scales, hp1,
 
         w_scales = sb.tile([P, 3, M], U8, name="w_scales", align_bytes=64)
         w_words = [sb.tile([P, 2 * M], U8, name=f"w_words{w}", align_bytes=64) for w in range(3)]
-        raw = [sb.tile([P, PACK, N], F32, name=f"raw{a}") for a in range(2)]
+        raw_x = [sb.tile([P, PACK, N // 2], F32, name=f"raw_x{a}") for a in range(2)]
+        raw_dy = sb.tile([P, PACK, N], F32, name="raw_dy")
         packed = [sb.tile([P, N, PACK], BF16, name=f"packed{a}", align_bytes=64) for a in range(2)]
         codes = [sb.tile([P, N], U32, name=f"codes{a}", align_bytes=64) for a in range(2)]
         scales = [sb.tile([P, N], U8, name=f"scales{a}", align_bytes=64) for a in range(2)]
@@ -61,12 +62,12 @@ def tile_rows_bhill_kernel(tc, x, w1_words, w1_scales, w2_words, w2_scales, hp1,
                     out=w_scales[32 * quad : 32 * quad + 4, w, :].bitcast(I32), in_=rows[4 * quad : 4 * quad + 4, :]
                 )
 
-        def load_act(k, src):
-            nc.sync.dma_start(out=raw[k][:], in_=src.rearrange("g (p j) n -> (g p) j n", j=PACK))
+        def load_act(dst, src):
+            nc.sync.dma_start(out=dst[:], in_=src.rearrange("g (p j) n -> (g p) j n", j=PACK))
 
-        def interleave_views(k, c0, c1):
+        def interleave_views(k, raw, first, c0, c1):
             dst = packed[k][:, c0:c1, :].rearrange("p (c i) j -> p c j i", i=4)
-            src = raw[k][:, :, c0:c1].rearrange("p j (c i) -> p c j i", i=4)
+            src = raw[:, :, c0 - first : c1 - first].rearrange("p j (c i) -> p c j i", i=4)
             return dst, src
 
         def quantize(k, c0, c1):
@@ -104,11 +105,12 @@ def tile_rows_bhill_kernel(tc, x, w1_words, w1_scales, w2_words, w2_scales, hp1,
         nc.scalar.activation(out=warm[:, 1:2], in_=warm[:, 0:1], func=ACT.Sigmoid)
 
         floor = warm[:, 1:2]
-        load_act(0, x)
+        load_act(raw_x[0], x[:, :, : N // 2])
+        load_act(raw_x[1], x[:, :, N // 2 :])
         load_words(0, w1_words)
         load_scales(0, w1_scales)
         load_words(1, w2_words)
-        load_act(1, dy)
+        load_act(raw_dy, dy)
         load_scales(1, w2_scales)
         load_words(2, wo_words)
         load_scales(2, wo_scales)
@@ -117,13 +119,16 @@ def tile_rows_bhill_kernel(tc, x, w1_words, w1_scales, w2_words, w2_scales, hp1,
         for t in range(HALVES):
             nc.sync.dma_start(out=old_sb[:, t], in_=old[:, P * t : P * (t + 1), :].rearrange("g p n -> p g n"))
 
-        for c0, c1 in ((0, N // 2), (N // 2, X_SPLIT)):
-            dst, src = interleave_views(0, c0, c1)
-            nc.vector.tensor_copy(out=dst, in_=src)
-        dst, src = interleave_views(0, X_SPLIT, N)
-        nc.scalar.copy(out=dst, in_=src)
+        dst, src = interleave_views(0, raw_x[0], 0, 0, N // 2)
+        nc.vector.tensor_copy(out=dst, in_=src)
         quantize(0, 0, N // 2)
-        quantize(0, N // 2, N)
+        for c0, c1 in ((N // 2, 3 * N // 4), (3 * N // 4, X_SPLIT)):
+            dst, src = interleave_views(0, raw_x[1], N // 2, c0, c1)
+            nc.vector.tensor_copy(out=dst, in_=src)
+        dst, src = interleave_views(0, raw_x[1], N // 2, X_SPLIT, N)
+        nc.scalar.copy(out=dst, in_=src)
+        quantize(0, N // 2, 3 * N // 4)
+        quantize(0, 3 * N // 4, N)
         tiles = range(len(TILES))
         late_first = [2, 3, 0, 1]
         for i in late_first:
@@ -133,7 +138,7 @@ def tile_rows_bhill_kernel(tc, x, w1_words, w1_scales, w2_words, w2_scales, hp1,
             product(bank2[i], i, 1, 0)
             nc.scalar.activation(out=t2[:, cols(i)], in_=bank2[i][:], func=ACT.Sigmoid, scale=-1.0)
 
-        dst, src = interleave_views(1, 0, N)
+        dst, src = interleave_views(1, raw_dy, 0, 0, N)
         nc.vector.tensor_copy(out=dst, in_=src)
         quantize(1, 0, N)
         c0_bank = {2: bank1[2], 3: bank1[3], 0: bank2[2], 1: bank2[3]}

from contextlib import ExitStack

import concourse.mybir as mybir

G, D, M, N = 2, 256, 256, 512
FLOPS = 3 * 2 * G * D * M * N

F32 = mybir.dt.float32
BF16 = mybir.dt.bfloat16
I32 = mybir.dt.int32
U32 = mybir.dt.uint32
U8 = mybir.dt.uint8
FP8X4 = mybir.dt.float8_e4m3fn_x4
FP4X4 = mybir.dt.float4_e2m1fn_x4
ACT = mybir.ActivationFunctionType
ALU = mybir.AluOpType

P = 128
PACK = 4
ROWS = D // PACK
HALVES = M // P
TILES = [(g, t) for t in range(HALVES) for g in range(G)]
CROSSOVER = 35.0
X_SPLIT = 416
POOL_COLS = 896


def tile_rows_bhill_kernel(tc, x, w1_words, w1_scales, w2_words, w2_scales, hp1, wo_words, wo_scales, dy, old, out):
    nc = tc.nc
    with ExitStack() as ctx:
        sb = ctx.enter_context(tc.tile_pool(name="sb", bufs=1))
        ps = ctx.enter_context(tc.psum_pool(name="ps", bufs=1))
        ctx.enter_context(tc.manual_schedule())

        def per_tile(name):
            return sb.tile([P, len(TILES) * N], F32, name=name)

        w_scales = sb.tile([P, 3, M], U8, name="w_scales", align_bytes=64)
        w_words = [sb.tile([P, 2 * M], U8, name=f"w_words{w}", align_bytes=64) for w in range(3)]
        raw_x = [sb.tile([P, PACK, N // 2], F32, name=f"raw_x{a}") for a in range(2)]
        raw_dy = sb.tile([P, PACK, N], F32, name="raw_dy")
        packed = [sb.tile([P, N, PACK], BF16, name=f"packed{a}", align_bytes=64) for a in range(2)]
        codes = [sb.tile([P, N], U32, name=f"codes{a}", align_bytes=64) for a in range(2)]
        scales = [sb.tile([P, N], U8, name=f"scales{a}", align_bytes=64) for a in range(2)]
        half_point = sb.tile([P, G * HALVES, 8], F32, name="half_point")
        old_sb = sb.tile([P, HALVES, G, N], F32, name="old_sb")
        warm = sb.tile([P, 2], F32, name="warm")
        bank1 = [ps.tile([P, N], F32, name=f"bank1_{i}") for i in range(len(TILES))]
        bank2 = [ps.tile([P, N], F32, name=f"bank2_{i}") for i in range(len(TILES))]
        t1, t2, l1, l2, n1, n2, q, den, lden, inv2, a, prod, b, dz, res = [
            per_tile(s)
            for s in ("t1", "t2", "l1", "l2", "n1", "n2", "q", "den", "lden", "inv2", "a", "prod", "b", "dz", "res")
        ]

        def load_words(w, words):
            nc.sync.dma_start(out=w_words[w][:].bitcast(I32), in_=words.rearrange("g p b -> (g p) b").bitcast(I32))

        def load_scales(w, scale_bytes):
            rows = scale_bytes.rearrange("g t m -> (g t) m").bitcast(I32)
            for quad in range(4):
                nc.sync.dma_start(
                    out=w_scales[32 * quad : 32 * quad + 4, w, :].bitcast(I32), in_=rows[4 * quad : 4 * quad + 4, :]
                )

        def load_act(dst, src):
            nc.sync.dma_start(out=dst[:], in_=src.rearrange("g (p j) n -> (g p) j n", j=PACK))

        def interleave_views(k, raw, first, c0, c1):
            dst = packed[k][:, c0:c1, :].rearrange("p (c i) j -> p c j i", i=4)
            src = raw[:, :, c0 - first : c1 - first].rearrange("p j (c i) -> p c j i", i=4)
            return dst, src

        def quantize(k, c0, c1):
            nc.vector.quantize_mx(
                out=codes[k][:, c0:c1].bitcast(FP8X4),
                scales=scales[k][:, c0:c1],
                in_=packed[k][:, c0:c1, :].rearrange("p n j -> p (n j)"),
            )

        def product(bank, i, w, k):
            g, t = TILES[i]
            rows = slice(ROWS * g, ROWS * (g + 1))
            nc.tensor.matmul_mx(
                out=bank[:],
                lhsT=w_words[w][rows, 2 * P * t : 2 * P * (t + 1)].bitcast(FP4X4),
                lhsT_scale=w_scales[rows, w, P * t : P * (t + 1)],
                rhs=codes[k][rows, :].bitcast(FP8X4),
                rhs_scale=scales[k][rows, :],
                start=True,
                stop=True,
            )

        def h(i):
            g, t = TILES[i]
            return half_point[:, HALVES * g + t, 0:1]

        def cols(i, c0=0, c1=N):
            return slice(i * N + c0, i * N + c1)

        def stt(dst, in0, scalar, in1, op0, op1):
            nc.vector.scalar_tensor_tensor(out=dst, in0=in0, scalar=scalar, in1=in1, op0=op0, op1=op1)

        nc.vector.memset(w_scales[:].rearrange("p w m -> p (w m)").bitcast(I32), 0)
        nc.vector.memset(warm[:, 0:1], -CROSSOVER)
        nc.scalar.activation(out=warm[:, 1:2], in_=warm[:, 0:1], func=ACT.Sigmoid)

        floor = warm[:, 1:2]
        load_act(raw_x[0], x[:, :, : N // 2])
        load_act(raw_x[1], x[:, :, N // 2 :])
        load_words(0, w1_words)
        load_scales(0, w1_scales)
        load_words(1, w2_words)
        load_act(raw_dy, dy)
        load_scales(1, w2_scales)
        load_words(2, wo_words)
        load_scales(2, wo_scales)
        with nc.allow_non_contiguous_dma(reason="one half point a partition"):
            nc.sync.dma_start(out=half_point[:, :, 0:1], in_=hp1.rearrange("g (t p) o -> p (g t) o", p=P))
        for t in range(HALVES):
            nc.sync.dma_start(out=old_sb[:, t], in_=old[:, P * t : P * (t + 1), :].rearrange("g p n -> p g n"))

        dst, src = interleave_views(0, raw_x[0], 0, 0, N // 2)
        nc.vector.tensor_copy(out=dst, in_=src)
        quantize(0, 0, N // 2)
        for c0, c1 in ((N // 2, 3 * N // 4), (3 * N // 4, X_SPLIT)):
            dst, src = interleave_views(0, raw_x[1], N // 2, c0, c1)
            nc.vector.tensor_copy(out=dst, in_=src)
        dst, src = interleave_views(0, raw_x[1], N // 2, X_SPLIT, N)
        nc.scalar.copy(out=dst, in_=src)
        quantize(0, N // 2, 3 * N // 4)
        quantize(0, 3 * N // 4, N)
        tiles = range(len(TILES))
        late_first = [2, 3, 0, 1]
        for i in late_first:
            product(bank1[i], i, 0, 0)
            nc.scalar.activation(out=t1[:, cols(i)], in_=bank1[i][:], func=ACT.Sigmoid, scale=-1.0)
        for i in late_first:
            product(bank2[i], i, 1, 0)
            nc.scalar.activation(out=t2[:, cols(i)], in_=bank2[i][:], func=ACT.Sigmoid, scale=-1.0)

        dst, src = interleave_views(1, raw_dy, 0, 0, N)
        nc.vector.tensor_copy(out=dst, in_=src)
        quantize(1, 0, N)
        c0_bank = {2: bank1[2], 3: bank1[3], 0: bank2[2], 1: bank2[3]}
        for i in late_first:
            product(c0_bank[i], i, 2, 1)
            stt(a[:, cols(i)], t1[:, cols(i)], 1.0, c0_bank[i][:], ALU.subtract, ALU.mult)
        for i in (2, 3):
            product(bank1[i], i, 0, 0)
        for i in (2, 3):
            product(bank2[i], i, 1, 0)

        old_flat = old_sb[:].rearrange("p t g n -> p (t g n)")

        def s_ln(dst, src, where, bias):
            nc.scalar.activation(out=dst[:, where], in_=src[:, where], func=ACT.Ln, bias=bias)

        def v_min(dst, bank, src, i, c0=0, c1=N):
            stt(dst[:, cols(i, c0, c1)], bank[i][:, c0:c1], -1.0, src[:, cols(i, c0, c1)], ALU.mult, ALU.min)

        def mul(engine, dst, in0, in1, where):
            engine.tensor_tensor(out=dst[:, where], in0=in0[:, where], in1=in1[:, where], op=ALU.mult)

        def s_inv2(where):
            nc.scalar.activation(out=inv2[:, where], in_=lden[:, where], func=ACT.Exp, scale=-2.0)

        def v_dz(where):
            stt(dz[:, where], b[:, where], -4.0, inv2[:, where], ALU.mult, ALU.mult)

        def v_res(i, c0=0, c1=N):
            g, t = TILES[i]
            where = cols(i, c0, c1)
            nc.vector.tensor_tensor(out=res[:, where], in0=dz[:, where], in1=old_flat[:, where], op=ALU.add)
            nc.sync.dma_start(out=out[g, P * t : P * (t + 1), c0:c1], in_=res[:, where])

        count = len(TILES)
        for i in tiles:
            for c0, c1 in [(0, N // 2), (N // 2, N)] if i == 0 else [(0, N)]:
                s_ln(l1, t1, cols(i, c0, c1), floor)
                v_min(n1, bank1, l1, i, c0, c1)
        mul(nc.gpsimd, q, n1, n1, cols(0))
        mul(nc.gpsimd, prod, a, n1, slice(0, POOL_COLS))
        for i in tiles:
            s_ln(l2, t2, cols(i), floor)
            v_min(n2, bank2, l2, i)
        for i in tiles:
            if i > 0:
                nc.scalar.activation(out=q[:, cols(i)], in_=n1[:, cols(i)], func=ACT.Square)
            stt(den[:, cols(i)], q[:, cols(i)], h(i), n2[:, cols(i)], ALU.add, ALU.subtract)
        for i in tiles:
            s_ln(lden, den, cols(i), 0.0)
        mul(nc.vector, prod, a, n1, slice(POOL_COLS, count * N))
        for i in tiles:
            stt(b[:, cols(i)], n2[:, cols(i)], h(i), prod[:, cols(i)], ALU.subtract, ALU.mult)
        halves = [(0, N // 2), (N // 2, N)]
        last = count - 1
        for i in tiles:
            for c0, c1 in halves if i == 0 else [(0, N)]:
                s_inv2(cols(i, c0, c1))
        for c0, c1 in halves:
            v_dz(cols(0, c0, c1))
        for i in range(1, last):
            v_dz(cols(i))
            v_res(i - 1)
        v_dz(cols(last, *halves[0]))
        v_res(last - 1)
        v_dz(cols(last, *halves[1]))
        for c0, c1 in halves:
            v_res(last, c0, c1)
